import numpy as np
import ml_dtypes


def mxq(x, axis, fmt="e4m3"):
    dtype, down = {"e4m3": (ml_dtypes.float8_e4m3fn, 7), "e5m2": (ml_dtypes.float8_e5m2, 14)}[fmt]
    v = np.moveaxis(np.asarray(x, np.float32).astype(ml_dtypes.bfloat16).astype(np.float64), axis, -1)
    blocks = v.reshape(v.shape[:-1] + (-1, 32))
    amax = np.abs(blocks).max(-1, keepdims=True)
    byte = np.maximum(np.where(amax > 0, np.frexp(amax)[1] - 1 + 127, 0) - down, 1)
    scale = np.exp2(byte - 127.0)
    codes = (blocks / scale).astype(np.float32).astype(dtype).astype(np.float64)
    return np.moveaxis((codes * scale).reshape(v.shape), -1, axis)


WIDE = False


def mx_kscale(k):
    if not WIDE:
        return np.ones(k)
    levels = np.array([10, -10, 5, -5, 0])
    if k % 512:
        return np.exp2(np.random.permutation(np.resize(levels, k // 32))).repeat(32)
    a = np.empty((k // 512, 16))
    for p in range(k // 512):
        a[p, :8] = np.random.permutation(np.resize(levels, 8))
        for g in range(8):
            far = levels[np.abs(levels - a[p, g]) >= 10]
            a[p, g + 8] = far[np.random.randint(len(far))]
    return np.exp2(a.ravel()).repeat(32)


BF16 = ml_dtypes.bfloat16


def bf(x):
    return np.asarray(x, np.float32).astype(BF16)


def f64(x):
    return np.asarray(x).astype(np.float64)


E2M1 = np.array([0.0, 0.5, 1.0, 1.5, 2.0, 3.0, 4.0, 6.0, -0.0, -0.5, -1.0, -1.5, -2.0, -3.0, -4.0, -6.0])


def pack_weight(w, fmt):
    k, n = w.shape
    w = f64(bf(w)).reshape(k // 32, 32, n)
    amax = np.abs(w).max(1)
    if fmt == "e4m3":
        byte = np.frexp(amax)[1] - 1 + 127 - 7
    else:
        mant, ex = np.frexp(amax / 6.0)
        byte = np.where(mant > 0.5, ex, ex - 1) + 127
    byte = np.clip(np.where(amax > 0, byte, 1), 1, 254)
    scaled = (w * np.exp2(127.0 - byte)[:, None, :]).reshape(k, n).astype(np.float32)
    by_word = np.ascontiguousarray(scaled.reshape(k // 512, 128, 4, n).transpose(0, 1, 3, 2))
    if fmt == "e4m3":
        words = by_word.astype(ml_dtypes.float8_e4m3fn).view(np.uint8)
    else:
        c = by_word.astype(ml_dtypes.float4_e2m1fn).view(np.uint8) & 0xF
        words = c[..., 0::2] | (c[..., 1::2] << 4)
    return np.ascontiguousarray(words), np.ascontiguousarray(byte.astype(np.uint8).reshape(k // 512, 16, n))


def unpack_weight(words, scales, fmt):
    g, p, n, _ = words.shape
    if fmt == "e4m3":
        vals = np.ascontiguousarray(words).view(ml_dtypes.float8_e4m3fn).astype(np.float64)
    else:
        nib = np.empty((g, p, n, 4), np.uint8)
        nib[..., 0::2] = words & 0xF
        nib[..., 1::2] = words >> 4
        vals = E2M1[nib]
    vals = vals * np.repeat(np.exp2(scales.astype(np.float64) - 127.0), 8, axis=1)[..., None]
    return vals.transpose(0, 1, 3, 2).reshape(g * 512, n)
def pack4(w):
    words, scales = pack_weight(w, "e2m1")
    return words.reshape(words.shape[0], 128, -1), scales


def unpack4(words, scales):
    return unpack_weight(words.reshape(words.shape[0], 128, -1, 2), scales, "e2m1")


def planes(Y):
    n, m = Y.shape
    b = f64(bf(Y)).reshape(n // 32, 32, m)
    amax = np.abs(b).max(1)
    byte = np.clip(np.where(amax > 0, np.frexp(amax)[1] - 1 + 127 - 7, 1), 1, 254)
    codes = (b * np.exp2(127.0 - byte)[:, None, :]).reshape(n, m).astype(np.float32).astype(ml_dtypes.float8_e4m3fn).view(np.uint8)
    words = codes.reshape(n // 512, 128, 4, m).transpose(0, 1, 3, 2)
    return np.ascontiguousarray(words), np.ascontiguousarray(byte.astype(np.uint8).reshape(n // 512, 16, m))


P, T, F, J, K = 2048, 8, 128, 8, 1024
S, N = T * F, J * F

def high_pass(r):
    return 1.0 - 0.7 / (1.0 + np.exp((r - 0.4) / 0.1))

def setup_inputs():
    s, t = mx_kscale(K), mx_kscale(S)
    spread = np.exp(0.5 * np.random.randn(F))
    D = np.random.randn(K, P * T) * s[:, None]
    C = np.random.randn(K, F) / np.sqrt(K) * spread[None, :] / s[:, None]
    gain = np.exp(0.2 * np.random.randn(T, F)) / spread[None, :] * t.reshape(T, F)
    radius = np.random.rand(P, 1)
    src = high_pass(np.abs(radius + 0.05 * np.random.randn(P, T)))
    unf = 1.0 / high_pass(np.abs(radius + 0.05 * np.random.randn(P, J)))
    W = np.random.randn(S, N) / np.sqrt(S) * np.exp(0.8 * np.random.randn(N))[None, :] / t[:, None]
    d_words, d_scales = pack4(D)
    c_words, c_scales = pack4(C)
    return {"d_words": d_words, "d_scales": d_scales, "c_words": c_words, "c_scales": c_scales,
            "source_filter": bf(src), "gain": bf(gain), "kernel": bf(W), "unfilter": bf(unf)}

def reference(d_words, d_scales, c_words, c_scales, source_filter, gain, kernel, unfilter):
    D = unpack4(d_words, d_scales)
    C = unpack4(c_words, c_scales)
    V = D.T @ C
    X = V.reshape(P, T, F) * f64(source_filter)[:, :, None] * f64(gain)[None, :, :]
    X = X.reshape(P, S)
    Z = mxq(X, 1, "e4m3") @ mxq(f64(kernel), 0, "e4m3")
    y = (Z.reshape(P, J, F) * f64(unfilter)[:, :, None]).reshape(P, N)
    Y = y.T
    words, scales = planes(Y)
    return y, words, scales

@@ -1,0 +1,314 @@
+from contextlib import ExitStack
+
+import concourse.mybir as mybir
+from concourse.masks import make_identity
+
+F32 = mybir.dt.float32
+BF16 = mybir.dt.bfloat16
+U32 = mybir.dt.uint32
+I32 = mybir.dt.int32
+U8 = mybir.dt.uint8
+FP8X4 = mybir.dt.float8_e4m3fn_x4
+FP4X4 = mybir.dt.float4_e2m1fn_x4
+COPY = mybir.ActivationFunctionType.Copy
+MULT = mybir.AluOpType.mult
+
+P = 128
+A_ALL, TAPS, CH, POS, K1 = 2048, 8, 128, 8, 1024
+S_LEN, N_OUT = TAPS * CH, POS * CH
+FLOPS = 2 * K1 * A_ALL * TAPS * CH + 2 * A_ALL * S_LEN * N_OUT
+CHUNKS = A_ALL // P
+ROWS = P * TAPS
+BANK = 512
+
+LAG_MM2 = 5
+D_RING, D_AHEAD = 8, 6
+SCALE_RANGES = [(0, 2, 0, -1), (2, 6, 1, -1), (6, 10, 2, -1), (10, 14, 1, 6), (14, 16, 0, 9)]
+WORD_GROUPS = [(0, 4), (4, 8), (8, 12), (12, 14), (14, 16)]
+SCALE_GROUPS = [(0, 8), (8, 16)]
+
+
+def tile_coil_compress_grappa_planes_k5_kernel(
+    tc, d_words, d_scales, c_words, c_scales, source_filter, gain, kernel, unfilter, out_0, out_1, out_2
+):
+    nc = tc.nc
+    with ExitStack() as ctx:
+        sb = ctx.enter_context(tc.tile_pool(name="sb", bufs=1))
+        ps = ctx.enter_context(tc.psum_pool(name="ps", bufs=1))
+
+        def ring(name, count, shape, dtype):
+            return [sb.tile(shape, dtype, name="%s%d" % (name, n), align_bytes=64) for n in range(count)]
+
+        def banks(name, count):
+            return [ps.tile([P, BANK], F32, name="%s%d" % (name, n)) for n in range(count)]
+
+        bank_v, bank_vt, bank_z = banks("bank_v", 2), banks("bank_vt", 2), banks("bank_z", 2)
+        bank_xt, bank_yt = banks("bank_xt", 1)[0], banks("bank_yt", 1)[0]
+
+        dw = ring("dw", D_RING, [P, 2, 2 * ROWS], U8)
+        dsc = [
+            sb.tile([P, 2, n * ROWS], U8, name="dsc%d" % j, align_bytes=64) for j, n in enumerate((2, 4, 4))
+        ]
+        cw = sb.tile([P, 2, 2 * CH], U8, align_bytes=64)
+        csc = sb.tile([P, 2, CH], U8, align_bytes=64)
+        ident = sb.tile([P, P], F32, align_bytes=64)
+        gain_rows = sb.tile([TAPS, CH], BF16, align_bytes=64)
+        gain_pad = sb.tile([P, CH], F32, align_bytes=64)
+        gain_t = sb.tile([P, TAPS, 1], F32, align_bytes=64)
+        src_bf = sb.tile([P, CHUNKS, TAPS], BF16, align_bytes=64)
+        unf_bf = sb.tile([P, CHUNKS, POS], BF16, align_bytes=64)
+        src = sb.tile([P, CHUNKS * TAPS], F32, align_bytes=64)
+        unf = sb.tile([P, CHUNKS * POS], F32, align_bytes=64)
+        w_raw = ring("w_raw", 2, [P, 4, N_OUT], BF16)
+        w_grp = ring("w_grp", 4, [P, BANK, 4], BF16)
+        wq = ring("wq", 4, [P, BANK], U32)
+        ws = ring("ws", 4, [P, BANK], U8)
+        vt = ring("vt", 3, [P, TAPS, P], F32)
+        xb = ring("xb", 6, [P, BANK], BF16)
+        xg = ring("xg", 2, [P, 2 * BANK], BF16)
+        xq = ring("xq", 4, [P, 2 * P], U32)
+        xs = ring("xs", 4, [P, 2 * P], U8)
+        y = ring("y", 4, [P, N_OUT], F32)
+        yb = ring("yb", 6, [P, BANK], BF16)
+        yg = ring("yg", 2, [P, 2 * BANK], BF16)
+        yq = [
+            sb.tile([P, 2, (hi - lo) * P], U32, name="yq%d" % lo, align_bytes=64) for lo, hi in WORD_GROUPS
+        ]
+        ys = [
+            sb.tile([P, 2, (hi - lo) * P], U8, name="ys%d" % lo, align_bytes=64) for lo, hi in SCALE_GROUPS
+        ]
+
+        def group_of(groups, c):
+            return [n for n, grp in enumerate(groups) if grp[0] <= c < grp[1]][0]
+
+        def load_d(c):
+            nc.sync.dma_start(
+                out=dw[c % D_RING][:].bitcast(I32),
+                in_=d_words[:, :, 2 * ROWS * c : 2 * ROWS * (c + 1)].rearrange("g p n -> p g n").bitcast(I32),
+            )
+
+        def scale_rows(dram, r):
+            return dram.rearrange("g (q r) n -> r q g n", r=4)[r].bitcast(I32)
+
+        def load_d_scales(n):
+            lo, hi, slot = SCALE_RANGES[n][:3]
+            for r in range(4):
+                nc.sync.dma_start(
+                    out=dsc[slot][r:P:32, :, :].bitcast(I32),
+                    in_=scale_rows(d_scales[:, :, ROWS * lo : ROWS * hi], r),
+                )
+
+        def load_w(g):
+            nc.sync.dma_start(
+                out=w_raw[g][:], in_=kernel[BANK * g : BANK * (g + 1), :].rearrange("(p t) n -> p t n", t=4)
+            )
+
+        def interleave_w(g, h, copy):
+            copy(
+                out=w_grp[2 * g + h][:].rearrange("p (c i) t -> p c t i", i=4),
+                in_=w_raw[g][:, :, BANK * h : BANK * (h + 1)].rearrange("p t (c i) -> p c t i", i=4),
+            )
+
+        def quantize_w(g, h):
+            n = 2 * g + h
+            nc.vector.quantize_mx(
+                out=wq[n][:].bitcast(FP8X4), scales=ws[n][:], in_=w_grp[n][:].rearrange("p n t -> p (n t)")
+            )
+
+        def compress(c, h):
+            lo, hi, slot = SCALE_RANGES[group_of(SCALE_RANGES, c)][:3]
+            col = ROWS * (c - lo) + BANK * h
+            for g in range(2):
+                nc.tensor.matmul_mx(
+                    out=bank_v[h][:],
+                    lhsT=cw[:, g, :].bitcast(FP4X4),
+                    lhsT_scale=csc[:, g, :],
+                    rhs=dw[c % D_RING][:, g, 2 * BANK * h : 2 * BANK * (h + 1)].bitcast(FP4X4),
+                    rhs_scale=dsc[slot][:, g, col : col + BANK],
+                    start=(g == 0),
+                    stop=(g == 1),
+                )
+
+        def apply_gain(c, h):
+            nc.vector.tensor_tensor(
+                out=vt[c % 3][:, :, 64 * h : 64 * (h + 1)],
+                in0=bank_v[h][:].rearrange("p (a b) -> p b a", b=TAPS),
+                in1=gain_t[:].to_broadcast([P, TAPS, 64]),
+                op=MULT,
+            )
+
+        def turn_v(c):
+            for b in range(TAPS):
+                nc.tensor.transpose(bank_vt[b // 4][:, P * (b % 4) : P * (b % 4 + 1)], vt[c % 3][:, b, :], ident[:])
+
+        def apply_source_filter(c):
+            for b in range(TAPS):
+                g, b4 = divmod(b, 4)
+                nc.scalar.activation(
+                    out=xb[(2 * c + g) % 6][:].rearrange("p (e b m u) -> p b e m u", e=2, b=4, u=2)[:, b4],
+                    in_=bank_vt[g][:, P * b4 : P * (b4 + 1)].rearrange("p (m e u) -> p e m u", e=2, u=2),
+                    func=COPY,
+                    scale=src[:, TAPS * c + b : TAPS * c + b + 1],
+                )
+
+        def turn_words(bank, halves):
+            for g in range(2):
+                words = halves[g][:].bitcast(F32)
+                for e in range(2):
+                    n = 2 * g + e
+                    nc.tensor.transpose(bank[:, P * n : P * (n + 1)], words[:, P * e : P * (e + 1)], ident[:])
+
+        def gather_words(copy, dst, bank):
+            copy(
+                out=dst[:].bitcast(F32).rearrange("p (g a e) -> p g a e", g=2, e=2),
+                in_=bank[:].rearrange("p (g e a) -> p g a e", g=2, e=2),
+            )
+
+        def quantize_x(c):
+            nc.vector.quantize_mx(out=xq[c % 4][:].bitcast(FP8X4), scales=xs[c % 4][:], in_=xg[c % 2][:])
+
+        def predict(c, h):
+            for g in range(2):
+                nc.tensor.matmul_mx(
+                    out=bank_z[h][:],
+                    lhsT=xq[c % 4][:, P * g : P * (g + 1)].bitcast(FP8X4),
+                    lhsT_scale=xs[c % 4][:, P * g : P * (g + 1)],
+                    rhs=wq[2 * g + h][:].bitcast(FP8X4),
+                    rhs_scale=ws[2 * g + h][:],
+                    start=(g == 0),
+                    stop=(g == 1),
+                )
+
+        def apply_unfilter(c, h):
+            for j4 in range(4):
+                j = 4 * h + j4
+                nc.scalar.activation(
+                    out=y[c % 4][:, CH * j : CH * (j + 1)],
+                    in_=bank_z[h][:, CH * j4 : CH * (j4 + 1)],
+                    func=COPY,
+                    scale=unf[:, POS * c + j : POS * c + j + 1],
+                )
+
+        def round_y(c, g):
+            nc.vector.tensor_copy(
+                out=yb[(2 * c + g) % 6][:].rearrange("p (e o i u) -> p o e i u", e=2, i=4, u=2),
+                in_=y[c % 4][:, BANK * g : BANK * (g + 1)].rearrange("p (o i e u) -> p o e i u", e=2, i=4, u=2),
+            )
+
+        def quantize_y(c):
+            nw, ns = group_of(WORD_GROUPS, c), group_of(SCALE_GROUPS, c)
+            cw0, cs0 = P * (c - WORD_GROUPS[nw][0]), P * (c - SCALE_GROUPS[ns][0])
+            for g in range(2):
+                nc.vector.quantize_mx(
+                    out=yq[nw][:, g, cw0 : cw0 + P].bitcast(FP8X4),
+                    scales=ys[ns][:, g, cs0 : cs0 + P],
+                    in_=yg[c % 2][:, BANK * g : BANK * (g + 1)],
+                )
+
+        def store_y(c):
+            nc.sync.dma_start(out=out_0[P * c : P * (c + 1), :], in_=y[c % 4][:])
+
+        def store_planes(c):
+            nw, ns = group_of(WORD_GROUPS, c), group_of(SCALE_GROUPS, c)
+            lo, hi = WORD_GROUPS[nw]
+            if c == hi - 1:
+                nc.sync.dma_start(
+                    out=out_1[:, :, P * lo : P * hi, :].rearrange("g p m t -> p g (m t)").bitcast(I32),
+                    in_=yq[nw][:].bitcast(I32),
+                )
+            lo, hi = SCALE_GROUPS[ns]
+            if c == hi - 1:
+                for r in range(4):
+                    nc.sync.dma_start(
+                        out=scale_rows(out_2[:, :, P * lo : P * hi], r), in_=ys[ns][r:P:32, :, :].bitcast(I32)
+                    )
+
+        def live(c):
+            return 0 <= c < CHUNKS
+
+        ctx.enter_context(tc.manual_schedule())
+
+        nc.vector.memset(dsc[0][:].bitcast(I32), 0)
+        nc.vector.memset(csc[:].bitcast(I32), 0)
+        nc.vector.memset(gain_pad[:], 0.0)
+        nc.gpsimd.dma_start(out=gain_rows[:], in_=gain[:, :])
+        nc.gpsimd.dma_start(out=cw[:].bitcast(I32), in_=c_words.rearrange("g p n -> p g n").bitcast(I32))
+        nc.gpsimd.dma_start(out=csc[3:P:32, :, :].bitcast(I32), in_=scale_rows(c_scales, 3))
+        make_identity(nc, ident[:])
+        nc.gpsimd.memset(dsc[1][:].bitcast(I32), 0)
+        nc.gpsimd.memset(dsc[2][:].bitcast(I32), 0)
+
+        load_d(0)
+        load_d_scales(0)
+        for r in range(3):
+            nc.sync.dma_start(out=csc[r:P:32, :, :].bitcast(I32), in_=scale_rows(c_scales, r))
+        load_d(1)
+        nc.sync.dma_start(out=src_bf[:], in_=source_filter.rearrange("(c p) b -> p c b", p=P))
+        load_d(2)
+        load_d_scales(1)
+        load_w(0)
+        load_d(3)
+        load_w(1)
+        load_d(4)
+        nc.sync.dma_start(out=unf_bf[:], in_=unfilter.rearrange("(c p) j -> p c j", p=P))
+        load_d(5)
+        load_d_scales(2)
+
+        nc.scalar.activation(out=gain_pad[0:TAPS, :], in_=gain_rows[:], func=COPY)
+        nc.tensor.transpose(bank_xt[:, 0:P], gain_pad[:], ident[:])
+        nc.vector.tensor_copy(out=gain_t[:, :, 0], in_=bank_xt[:, 0:TAPS])
+        nc.scalar.activation(out=src[:], in_=src_bf[:].rearrange("p c b -> p (c b)"), func=COPY)
+
+        for i in range(CHUNKS + LAG_MM2 + 2):
+            c_x, c_q, c_z, c_t, c_o = i - 2, i - 3, i - LAG_MM2, i - LAG_MM2 - 1, i - LAG_MM2 - 2
+            if live(i + D_AHEAD):
+                load_d(i + D_AHEAD)
+            for n, rng in enumerate(SCALE_RANGES):
+                if rng[3] == i:
+                    load_d_scales(n)
+            if live(c_x):
+                apply_source_filter(c_x)
+            if live(c_q):
+                gather_words(nc.vector.tensor_copy, xg[c_q % 2], bank_xt)
+            if live(c_o):
+                gather_words(nc.scalar.copy, yg[c_o % 2], bank_yt)
+            if live(i):
+                compress(i, 0)
+                compress(i, 1)
+                apply_gain(i, 0)
+            if live(c_q):
+                quantize_x(c_q)
+            if live(i):
+                apply_gain(i, 1)
+            if live(c_o):
+                quantize_y(c_o)
+            if i == 2:
+                interleave_w(0, 0, nc.scalar.copy)
+                interleave_w(0, 1, nc.vector.tensor_copy)
+            if i == 3:
+                interleave_w(1, 0, nc.scalar.copy)
+                quantize_w(0, 0)
+                quantize_w(0, 1)
+                interleave_w(1, 1, nc.vector.tensor_copy)
+            if i == 4:
+                quantize_w(1, 1)
+                quantize_w(1, 0)
+                nc.scalar.activation(out=unf[:], in_=unf_bf[:].rearrange("p c j -> p (c j)"), func=COPY)
+            if live(c_t):
+                store_y(c_t)
+            if live(c_z):
+                predict(c_z, 0)
+                predict(c_z, 1)
+                apply_unfilter(c_z, 0)
+                apply_unfilter(c_z, 1)
+            if live(i - 1):
+                turn_v(i - 1)
+            if live(c_x):
+                turn_words(bank_xt, [xb[(2 * c_x + g) % 6] for g in range(2)])
+            if live(c_t):
+                turn_words(bank_yt, [yb[(2 * c_t + g) % 6] for g in range(2)])
+            if live(c_z):
+                round_y(c_z, 0)
+                round_y(c_z, 1)
+            if live(c_o):
+                store_planes(c_o)

@@ -12,6 +12,7 @@ FP8X4 = mybir.dt.float8_e4m3fn_x4
 FP4X4 = mybir.dt.float4_e2m1fn_x4
 COPY = mybir.ActivationFunctionType.Copy
 MULT = mybir.AluOpType.mult
+ADD = mybir.AluOpType.add
 
 P = 128
 A_ALL, TAPS, CH, POS, K1 = 2048, 8, 128, 8, 1024
@@ -21,11 +22,13 @@ CHUNKS = A_ALL // P
 ROWS = P * TAPS
 BANK = 512
 
-LAG_MM2 = 5
-D_RING, D_AHEAD = 8, 6
-SCALE_RANGES = [(0, 2, 0, -1), (2, 6, 1, -1), (6, 10, 2, -1), (10, 14, 1, 6), (14, 16, 0, 9)]
-WORD_GROUPS = [(0, 4), (4, 8), (8, 12), (12, 14), (14, 16)]
-SCALE_GROUPS = [(0, 8), (8, 16)]
+LAG = 7
+XQ_RING = LAG - 1
+D_RING, D_AHEAD = 8, 5
+SC_RING = 3
+Y_RING = 5
+WORD_GROUPS = [(0, 4), (4, 8), (8, 11), (11, 13), (13, 15), (15, 16)]
+SCALE_GROUPS = [(0, 9), (9, 16)]
 
 
 def tile_coil_compress_grappa_planes_k5_kernel(
@@ -46,19 +49,16 @@ def tile_coil_compress_grappa_planes_k5_kernel(
         bank_xt, bank_yt = banks("bank_xt", 1)[0], banks("bank_yt", 1)[0]
 
         dw = ring("dw", D_RING, [P, 2, 2 * ROWS], U8)
-        dsc = [
-            sb.tile([P, 2, n * ROWS], U8, name="dsc%d" % j, align_bytes=64) for j, n in enumerate((2, 4, 4))
-        ]
+        dsc = ring("dsc", SC_RING, [P, 2, 2 * ROWS], U8)
         cw = sb.tile([P, 2, 2 * CH], U8, align_bytes=64)
         csc = sb.tile([P, 2, CH], U8, align_bytes=64)
         ident = sb.tile([P, P], F32, align_bytes=64)
         gain_rows = sb.tile([TAPS, CH], BF16, align_bytes=64)
         gain_pad = sb.tile([P, CH], F32, align_bytes=64)
         gain_t = sb.tile([P, TAPS, 1], F32, align_bytes=64)
-        src_bf = sb.tile([P, CHUNKS, TAPS], BF16, align_bytes=64)
-        unf_bf = sb.tile([P, CHUNKS, POS], BF16, align_bytes=64)
-        src = sb.tile([P, CHUNKS * TAPS], F32, align_bytes=64)
-        unf = sb.tile([P, CHUNKS * POS], F32, align_bytes=64)
+        filt_rows = sb.tile([2 * CHUNKS, ROWS], BF16, align_bytes=64)
+        filt_words = sb.tile([P, 4, P], F32, align_bytes=64)
+        filt = sb.tile([P, 2 * CHUNKS, TAPS], F32, align_bytes=64)
         w_raw = ring("w_raw", 2, [P, 4, N_OUT], BF16)
         w_grp = ring("w_grp", 4, [P, BANK, 4], BF16)
         wq = ring("wq", 4, [P, BANK], U32)
@@ -66,11 +66,11 @@ def tile_coil_compress_grappa_planes_k5_kernel(
         vt = ring("vt", 3, [P, TAPS, P], F32)
         xb = ring("xb", 6, [P, BANK], BF16)
         xg = ring("xg", 2, [P, 2 * BANK], BF16)
-        xq = ring("xq", 4, [P, 2 * P], U32)
-        xs = ring("xs", 4, [P, 2 * P], U8)
-        y = ring("y", 4, [P, N_OUT], F32)
-        yb = ring("yb", 6, [P, BANK], BF16)
-        yg = ring("yg", 2, [P, 2 * BANK], BF16)
+        xq = ring("xq", XQ_RING, [P, 2 * P], U32)
+        xs = ring("xs", XQ_RING, [P, 2 * P], U8)
+        y = ring("y", Y_RING, [P, N_OUT], F32)
+        yb = ring("yb", 8, [P, BANK], BF16)
+        yg = ring("yg", 3, [P, 2 * BANK], BF16)
         yq = [
             sb.tile([P, 2, (hi - lo) * P], U32, name="yq%d" % lo, align_bytes=64) for lo, hi in WORD_GROUPS
         ]
@@ -90,24 +90,41 @@ def tile_coil_compress_grappa_planes_k5_kernel(
         def scale_rows(dram, r):
             return dram.rearrange("g (q r) n -> r q g n", r=4)[r].bitcast(I32)
 
-        def load_d_scales(n):
-            lo, hi, slot = SCALE_RANGES[n][:3]
-            for r in range(4):
-                nc.sync.dma_start(
-                    out=dsc[slot][r:P:32, :, :].bitcast(I32),
-                    in_=scale_rows(d_scales[:, :, ROWS * lo : ROWS * hi], r),
+        def load_d_scales(n, queues):
+            for r, queue in enumerate(queues):
+                queue.dma_start(
+                    out=dsc[n % SC_RING][r:P:32, :, :].bitcast(I32),
+                    in_=scale_rows(d_scales[:, :, 2 * ROWS * n : 2 * ROWS * (n + 1)], r),
                 )
+
+        def load_filters(queue):
+            queue.dma_start(out=filt_rows[0:CHUNKS, :], in_=source_filter.rearrange("(c a) b -> c (a b)", a=P))
+            queue.dma_start(
+                out=filt_rows[CHUNKS : 2 * CHUNKS, :], in_=unfilter.rearrange("(c a) j -> c (a j)", a=P)
+            )
 
         def load_w(g):
             nc.sync.dma_start(
                 out=w_raw[g][:], in_=kernel[BANK * g : BANK * (g + 1), :].rearrange("(p t) n -> p t n", t=4)
             )
 
-        def interleave_w(g, h, copy):
+        def gpsimd_copy(out, in_):
+            nc.gpsimd.tensor_scalar(out=out, in0=in_, scalar1=1.0, scalar2=0.0, op0=MULT, op1=ADD)
+
+        def interleave_w(g, q, copy):
+            h, lo = q // 2, 256 * (q % 2)
             copy(
-                out=w_grp[2 * g + h][:].rearrange("p (c i) t -> p c t i", i=4),
-                in_=w_raw[g][:, :, BANK * h : BANK * (h + 1)].rearrange("p t (c i) -> p c t i", i=4),
+                out=w_grp[2 * g + h][:, lo : lo + 256, :].rearrange("p (c i) t -> p c t i", i=4),
+                in_=w_raw[g][:, :, 256 * q : 256 * (q + 1)].rearrange("p t (c i) -> p c t i", i=4),
             )
+
+        def interleave_w_on_gpsimd(g, q):
+            for s in range(2):
+                n0 = 256 * q + P * s
+                gpsimd_copy(
+                    out=w_grp[2 * g + q // 2][:, n0 % BANK : n0 % BANK + P, :].rearrange("p (c i) t -> p c t i", i=4),
+                    in_=w_raw[g][:, :, n0 : n0 + P].rearrange("p t (c i) -> p c t i", i=4),
+                )
 
         def quantize_w(g, h):
             n = 2 * g + h
@@ -115,24 +132,50 @@ def tile_coil_compress_grappa_planes_k5_kernel(
                 out=wq[n][:].bitcast(FP8X4), scales=ws[n][:], in_=w_grp[n][:].rearrange("p n t -> p (n t)")
             )
 
+        def v_bank(c, h):
+            return bank_z[h] if c < LAG and c % 2 == 1 else bank_v[h]
+
+        def z_bank(c, h):
+            return bank_v[h] if c + LAG > CHUNKS and c % 2 == 1 else bank_z[h]
+
+        def yt_bank(c):
+            return bank_vt[0] if c + LAG > CHUNKS + 1 and c % 2 == 1 else bank_yt
+
         def compress(c, h):
-            lo, hi, slot = SCALE_RANGES[group_of(SCALE_RANGES, c)][:3]
-            col = ROWS * (c - lo) + BANK * h
+            col = ROWS * (c % 2) + BANK * h
             for g in range(2):
                 nc.tensor.matmul_mx(
-                    out=bank_v[h][:],
+                    out=v_bank(c, h)[:],
                     lhsT=cw[:, g, :].bitcast(FP4X4),
                     lhsT_scale=csc[:, g, :],
                     rhs=dw[c % D_RING][:, g, 2 * BANK * h : 2 * BANK * (h + 1)].bitcast(FP4X4),
-                    rhs_scale=dsc[slot][:, g, col : col + BANK],
+                    rhs_scale=dsc[c // 2 % SC_RING][:, g, col : col + BANK],
                     start=(g == 0),
                     stop=(g == 1),
                 )
 
+        def turn_gain():
+            nc.scalar.activation(out=gain_pad[0:TAPS, :], in_=gain_rows[:], func=COPY)
+            nc.tensor.transpose(bank_xt[:, 0:P], gain_pad[:], ident[:])
+            nc.vector.tensor_copy(out=gain_t[:, :, 0], in_=bank_xt[:, 0:TAPS])
+
+        def sort_filters():
+            nc.vector.tensor_copy(
+                out=filt_words[0 : 2 * CHUNKS], in_=filt_rows[:].bitcast(F32).rearrange("c (a n) -> c n a", n=4)
+            )
+
+        def turn_filters():
+            for n in range(4):
+                nc.tensor.transpose(bank_yt[:, P * n : P * (n + 1)], filt_words[:, n, :], ident[:])
+            nc.vector.tensor_copy(
+                out=filt[:].rearrange("p c (n u) -> p c n u", u=2),
+                in_=bank_yt[:].bitcast(BF16).rearrange("p (n c u) -> p c n u", n=4, u=2)[:, 0 : 2 * CHUNKS],
+            )
+
         def apply_gain(c, h):
             nc.vector.tensor_tensor(
                 out=vt[c % 3][:, :, 64 * h : 64 * (h + 1)],
-                in0=bank_v[h][:].rearrange("p (a b) -> p b a", b=TAPS),
+                in0=v_bank(c, h)[:].rearrange("p (a b) -> p b a", b=TAPS),
                 in1=gain_t[:].to_broadcast([P, TAPS, 64]),
                 op=MULT,
             )
@@ -148,7 +191,7 @@ def tile_coil_compress_grappa_planes_k5_kernel(
                     out=xb[(2 * c + g) % 6][:].rearrange("p (e b m u) -> p b e m u", e=2, b=4, u=2)[:, b4],
                     in_=bank_vt[g][:, P * b4 : P * (b4 + 1)].rearrange("p (m e u) -> p e m u", e=2, u=2),
                     func=COPY,
-                    scale=src[:, TAPS * c + b : TAPS * c + b + 1],
+                    scale=filt[:, c, b : b + 1],
                 )
 
         def turn_words(bank, halves):
@@ -165,34 +208,45 @@ def tile_coil_compress_grappa_planes_k5_kernel(
             )
 
         def quantize_x(c):
-            nc.vector.quantize_mx(out=xq[c % 4][:].bitcast(FP8X4), scales=xs[c % 4][:], in_=xg[c % 2][:])
+            nc.vector.quantize_mx(
+                out=xq[c % XQ_RING][:].bitcast(FP8X4), scales=xs[c % XQ_RING][:], in_=xg[c % 2][:]
+            )
 
         def predict(c, h):
             for g in range(2):
                 nc.tensor.matmul_mx(
-                    out=bank_z[h][:],
-                    lhsT=xq[c % 4][:, P * g : P * (g + 1)].bitcast(FP8X4),
-                    lhsT_scale=xs[c % 4][:, P * g : P * (g + 1)],
+                    out=z_bank(c, h)[:],
+                    lhsT=xq[c % XQ_RING][:, P * g : P * (g + 1)].bitcast(FP8X4),
+                    lhsT_scale=xs[c % XQ_RING][:, P * g : P * (g + 1)],
                     rhs=wq[2 * g + h][:].bitcast(FP8X4),
                     rhs_scale=ws[2 * g + h][:],
                     start=(g == 0),
                     stop=(g == 1),
                 )
 
-        def apply_unfilter(c, h):
+        def unfilter_on_scalar(c, h):
             for j4 in range(4):
                 j = 4 * h + j4
                 nc.scalar.activation(
-                    out=y[c % 4][:, CH * j : CH * (j + 1)],
-                    in_=bank_z[h][:, CH * j4 : CH * (j4 + 1)],
+                    out=y[c % Y_RING][:, CH * j : CH * (j + 1)],
+                    in_=z_bank(c, h)[:, CH * j4 : CH * (j4 + 1)],
                     func=COPY,
-                    scale=unf[:, POS * c + j : POS * c + j + 1],
+                    scale=filt[:, CHUNKS + c, j : j + 1],
                 )
+
+        def unfilter_on_vector(c, h):
+            factors = filt[:, CHUNKS + c, 4 * h : 4 * h + 4].rearrange("p (j o) -> p j o", o=1)
+            nc.vector.tensor_tensor(
+                out=y[c % Y_RING][:, BANK * h : BANK * (h + 1)].rearrange("p (j f) -> p j f", j=4),
+                in0=z_bank(c, h)[:].rearrange("p (j f) -> p j f", j=4),
+                in1=factors.to_broadcast([P, 4, CH]),
+                op=MULT,
+            )
 
         def round_y(c, g):
             nc.vector.tensor_copy(
-                out=yb[(2 * c + g) % 6][:].rearrange("p (e o i u) -> p o e i u", e=2, i=4, u=2),
-                in_=y[c % 4][:, BANK * g : BANK * (g + 1)].rearrange("p (o i e u) -> p o e i u", e=2, i=4, u=2),
+                out=yb[(2 * c + g) % 8][:].rearrange("p (e o i u) -> p o e i u", e=2, i=4, u=2),
+                in_=y[c % Y_RING][:, BANK * g : BANK * (g + 1)].rearrange("p (o i e u) -> p o e i u", e=2, i=4, u=2),
             )
 
         def quantize_y(c):
@@ -202,11 +256,11 @@ def tile_coil_compress_grappa_planes_k5_kernel(
                 nc.vector.quantize_mx(
                     out=yq[nw][:, g, cw0 : cw0 + P].bitcast(FP8X4),
                     scales=ys[ns][:, g, cs0 : cs0 + P],
-                    in_=yg[c % 2][:, BANK * g : BANK * (g + 1)],
+                    in_=yg[c % 3][:, BANK * g : BANK * (g + 1)],
                 )
 
         def store_y(c):
-            nc.sync.dma_start(out=out_0[P * c : P * (c + 1), :], in_=y[c % 4][:])
+            nc.sync.dma_start(out=out_0[P * c : P * (c + 1), :], in_=y[c % Y_RING][:])
 
         def store_planes(c):
             nw, ns = group_of(WORD_GROUPS, c), group_of(SCALE_GROUPS, c)
@@ -228,87 +282,92 @@ def tile_coil_compress_grappa_planes_k5_kernel(
 
         ctx.enter_context(tc.manual_schedule())
 
-        nc.vector.memset(dsc[0][:].bitcast(I32), 0)
         nc.vector.memset(csc[:].bitcast(I32), 0)
+        nc.vector.memset(dsc[0][:].bitcast(I32), 0)
         nc.vector.memset(gain_pad[:], 0.0)
-        nc.gpsimd.dma_start(out=gain_rows[:], in_=gain[:, :])
+        nc.vector.memset(dsc[1][:].bitcast(I32), 0)
+        nc.vector.memset(filt_words[32:64], 0.0)
+        nc.vector.memset(filt_words[64:P], 0.0)
+        nc.vector.memset(dsc[2][:].bitcast(I32), 0)
         nc.gpsimd.dma_start(out=cw[:].bitcast(I32), in_=c_words.rearrange("g p n -> p g n").bitcast(I32))
-        nc.gpsimd.dma_start(out=csc[3:P:32, :, :].bitcast(I32), in_=scale_rows(c_scales, 3))
-        make_identity(nc, ident[:])
-        nc.gpsimd.memset(dsc[1][:].bitcast(I32), 0)
-        nc.gpsimd.memset(dsc[2][:].bitcast(I32), 0)
-
+        nc.gpsimd.dma_start(out=gain_rows[:], in_=gain[:, :])
         load_d(0)
-        load_d_scales(0)
-        for r in range(3):
+        for r in range(4):
             nc.sync.dma_start(out=csc[r:P:32, :, :].bitcast(I32), in_=scale_rows(c_scales, r))
+        load_d_scales(0, [nc.sync] * 3 + [nc.gpsimd])
+        make_identity(nc, ident[:])
         load_d(1)
-        nc.sync.dma_start(out=src_bf[:], in_=source_filter.rearrange("(c p) b -> p c b", p=P))
+
+        load_filters(nc.sync)
+        load_d_scales(1, [nc.sync] * 4)
         load_d(2)
-        load_d_scales(1)
         load_w(0)
         load_d(3)
-        load_w(1)
+        load_d_scales(2, [nc.sync] * 4)
         load_d(4)
-        nc.sync.dma_start(out=unf_bf[:], in_=unfilter.rearrange("(c p) j -> p c j", p=P))
-        load_d(5)
-        load_d_scales(2)
+        load_w(1)
 
-        nc.scalar.activation(out=gain_pad[0:TAPS, :], in_=gain_rows[:], func=COPY)
-        nc.tensor.transpose(bank_xt[:, 0:P], gain_pad[:], ident[:])
-        nc.vector.tensor_copy(out=gain_t[:, :, 0], in_=bank_xt[:, 0:TAPS])
-        nc.scalar.activation(out=src[:], in_=src_bf[:].rearrange("p c b -> p (c b)"), func=COPY)
-
-        for i in range(CHUNKS + LAG_MM2 + 2):
-            c_x, c_q, c_z, c_t, c_o = i - 2, i - 3, i - LAG_MM2, i - LAG_MM2 - 1, i - LAG_MM2 - 2
+        for i in range(CHUNKS + LAG + 1 + 1):
+            c_x, c_q, c_z = i - 2, i - 3, i - LAG
+            c_t, c_o = c_z - 1, c_z - 1 - 1
             if live(i + D_AHEAD):
                 load_d(i + D_AHEAD)
-            for n, rng in enumerate(SCALE_RANGES):
-                if rng[3] == i:
-                    load_d_scales(n)
+            if i % 2 == 0 and i >= 2 and live(i + 4):
+                load_d_scales(i // 2 + 2, [nc.sync] * 4)
+
             if live(c_x):
                 apply_source_filter(c_x)
             if live(c_q):
-                gather_words(nc.vector.tensor_copy, xg[c_q % 2], bank_xt)
+                gather_words(nc.scalar.copy, xg[c_q % 2], bank_xt)
             if live(c_o):
-                gather_words(nc.scalar.copy, yg[c_o % 2], bank_yt)
+                gather_words(nc.scalar.copy, yg[c_o % 3], yt_bank(c_o))
+            if live(c_z - 1):
+                round_y(c_z - 1, 0)
+                round_y(c_z - 1, 1)
             if live(i):
                 compress(i, 0)
                 compress(i, 1)
+                if i == 0:
+                    turn_gain()
                 apply_gain(i, 0)
+                apply_gain(i, 1)
+            if i == 0:
+                sort_filters()
             if live(c_q):
                 quantize_x(c_q)
-            if live(i):
-                apply_gain(i, 1)
             if live(c_o):
                 quantize_y(c_o)
-            if i == 2:
-                interleave_w(0, 0, nc.scalar.copy)
-                interleave_w(0, 1, nc.vector.tensor_copy)
+            if i == 1:
+                interleave_w_on_gpsimd(0, 0)
+                interleave_w_on_gpsimd(0, 1)
+                interleave_w_on_gpsimd(0, 2)
+                interleave_w_on_gpsimd(0, 3)
             if i == 3:
-                interleave_w(1, 0, nc.scalar.copy)
                 quantize_w(0, 0)
-                quantize_w(0, 1)
-                interleave_w(1, 1, nc.vector.tensor_copy)
+                interleave_w_on_gpsimd(1, 0)
+                interleave_w_on_gpsimd(1, 1)
+                interleave_w(1, 2, nc.vector.tensor_copy)
             if i == 4:
-                quantize_w(1, 1)
+                quantize_w(0, 1)
+                interleave_w(1, 3, nc.vector.tensor_copy)
+            if i == 5:
                 quantize_w(1, 0)
-                nc.scalar.activation(out=unf[:], in_=unf_bf[:].rearrange("p c j -> p (c j)"), func=COPY)
-            if live(c_t):
-                store_y(c_t)
+                quantize_w(1, 1)
+
+            if live(c_z - 1):
+                store_y(c_z - 1)
             if live(c_z):
                 predict(c_z, 0)
                 predict(c_z, 1)
-                apply_unfilter(c_z, 0)
-                apply_unfilter(c_z, 1)
+                unfilter_on_scalar(c_z, 0)
+                unfilter_on_vector(c_z, 1)
             if live(i - 1):
                 turn_v(i - 1)
+            if i == 1:
+                turn_filters()
             if live(c_x):
                 turn_words(bank_xt, [xb[(2 * c_x + g) % 6] for g in range(2)])
             if live(c_t):
-                turn_words(bank_yt, [yb[(2 * c_t + g) % 6] for g in range(2)])
-            if live(c_z):
-                round_y(c_z, 0)
-                round_y(c_z, 1)
+                turn_words(yt_bank(c_t), [yb[(2 * c_t + g) % 8] for g in range(2)])
             if live(c_o):
                 store_planes(c_o)

@@ -22,10 +22,11 @@ CHUNKS = A_ALL // P
 ROWS = P * TAPS
 BANK = 512
 
-LAG = 7
+LAG = 9
 XQ_RING = LAG - 1
-D_RING, D_AHEAD = 8, 5
+D_RING, D_AHEAD = 8, 4
 SC_RING = 3
+W_AFTER = [2, 4, 5, 7]
 Y_RING = 5
 WORD_GROUPS = [(0, 4), (4, 8), (8, 11), (11, 13), (13, 15), (15, 16)]
 SCALE_GROUPS = [(0, 9), (9, 16)]
@@ -59,7 +60,7 @@ def tile_coil_compress_grappa_planes_k5_kernel(
         filt_rows = sb.tile([2 * CHUNKS, ROWS], BF16, align_bytes=64)
         filt_words = sb.tile([P, 4, P], F32, align_bytes=64)
         filt = sb.tile([P, 2 * CHUNKS, TAPS], F32, align_bytes=64)
-        w_raw = ring("w_raw", 2, [P, 4, N_OUT], BF16)
+        w_raw = ring("w_raw", 4, [P, 4, BANK], BF16)
         w_grp = ring("w_grp", 4, [P, BANK, 4], BF16)
         wq = ring("wq", 4, [P, BANK], U32)
         ws = ring("ws", 4, [P, BANK], U8)
@@ -82,10 +83,14 @@ def tile_coil_compress_grappa_planes_k5_kernel(
             return [n for n, grp in enumerate(groups) if grp[0] <= c < grp[1]][0]
 
         def load_d(c):
+            if c % 2 == 0 and c > 0:
+                load_d_scales(c // 2, [nc.sync] * 4)
             nc.sync.dma_start(
                 out=dw[c % D_RING][:].bitcast(I32),
                 in_=d_words[:, :, 2 * ROWS * c : 2 * ROWS * (c + 1)].rearrange("g p n -> p g n").bitcast(I32),
             )
+            if c in W_AFTER:
+                load_w(W_AFTER.index(c))
 
         def scale_rows(dram, r):
             return dram.rearrange("g (q r) n -> r q g n", r=4)[r].bitcast(I32)
@@ -103,10 +108,10 @@ def tile_coil_compress_grappa_planes_k5_kernel(
                 out=filt_rows[CHUNKS : 2 * CHUNKS, :], in_=unfilter.rearrange("(c a) j -> c (a j)", a=P)
             )
 
-        def load_w(g):
-            nc.sync.dma_start(
-                out=w_raw[g][:], in_=kernel[BANK * g : BANK * (g + 1), :].rearrange("(p t) n -> p t n", t=4)
-            )
+        def load_w(n):
+            g, h = divmod(n, 2)
+            rows = kernel[BANK * g : BANK * (g + 1), BANK * h : BANK * (h + 1)]
+            nc.sync.dma_start(out=w_raw[n][:], in_=rows.rearrange("(p t) n -> p t n", t=4))
 
         def gpsimd_copy(out, in_):
             nc.gpsimd.tensor_scalar(out=out, in0=in_, scalar1=1.0, scalar2=0.0, op0=MULT, op1=ADD)
@@ -115,7 +120,7 @@ def tile_coil_compress_grappa_planes_k5_kernel(
             h, lo = q // 2, 256 * (q % 2)
             copy(
                 out=w_grp[2 * g + h][:, lo : lo + 256, :].rearrange("p (c i) t -> p c t i", i=4),
-                in_=w_raw[g][:, :, 256 * q : 256 * (q + 1)].rearrange("p t (c i) -> p c t i", i=4),
+                in_=w_raw[2 * g + h][:, :, lo : lo + 256].rearrange("p t (c i) -> p c t i", i=4),
             )
 
         def interleave_w_on_gpsimd(g, q):
@@ -123,7 +128,7 @@ def tile_coil_compress_grappa_planes_k5_kernel(
                 n0 = 256 * q + P * s
                 gpsimd_copy(
                     out=w_grp[2 * g + q // 2][:, n0 % BANK : n0 % BANK + P, :].rearrange("p (c i) t -> p c t i", i=4),
-                    in_=w_raw[g][:, :, n0 : n0 + P].rearrange("p t (c i) -> p c t i", i=4),
+                    in_=w_raw[2 * g + q // 2][:, :, n0 % BANK : n0 % BANK + P].rearrange("p t (c i) -> p c t i", i=4),
                 )
 
         def quantize_w(g, h):
@@ -289,31 +294,26 @@ def tile_coil_compress_grappa_planes_k5_kernel(
         nc.vector.memset(filt_words[32:64], 0.0)
         nc.vector.memset(filt_words[64:P], 0.0)
         nc.vector.memset(dsc[2][:].bitcast(I32), 0)
-        nc.gpsimd.dma_start(out=cw[:].bitcast(I32), in_=c_words.rearrange("g p n -> p g n").bitcast(I32))
-        nc.gpsimd.dma_start(out=gain_rows[:], in_=gain[:, :])
-        load_d(0)
+        make_identity(nc, ident[:])
+        nc.sync.dma_start(out=cw[:].bitcast(I32), in_=c_words.rearrange("g p n -> p g n").bitcast(I32))
+        nc.sync.dma_start(out=gain_rows[:], in_=gain[:, :])
         for r in range(4):
             nc.sync.dma_start(out=csc[r:P:32, :, :].bitcast(I32), in_=scale_rows(c_scales, r))
-        load_d_scales(0, [nc.sync] * 3 + [nc.gpsimd])
-        make_identity(nc, ident[:])
+        load_d(0)
+        load_d_scales(0, [nc.sync] * 4)
         load_d(1)
 
         load_filters(nc.sync)
-        load_d_scales(1, [nc.sync] * 4)
-        load_d(2)
-        load_w(0)
-        load_d(3)
-        load_d_scales(2, [nc.sync] * 4)
-        load_d(4)
-        load_w(1)
+        for c in range(2, D_AHEAD):
+            load_d(c)
+
+        turn_gain()
 
         for i in range(CHUNKS + LAG + 1 + 1):
-            c_x, c_q, c_z = i - 2, i - 3, i - LAG
+            c_x, c_w, c_q, c_z = i - 2, i - 3, i - 4, i - LAG
             c_t, c_o = c_z - 1, c_z - 1 - 1
             if live(i + D_AHEAD):
                 load_d(i + D_AHEAD)
-            if i % 2 == 0 and i >= 2 and live(i + 4):
-                load_d_scales(i // 2 + 2, [nc.sync] * 4)
 
             if live(c_x):
                 apply_source_filter(c_x)
@@ -327,8 +327,6 @@ def tile_coil_compress_grappa_planes_k5_kernel(
             if live(i):
                 compress(i, 0)
                 compress(i, 1)
-                if i == 0:
-                    turn_gain()
                 apply_gain(i, 0)
                 apply_gain(i, 1)
             if i == 0:
@@ -337,21 +335,23 @@ def tile_coil_compress_grappa_planes_k5_kernel(
                 quantize_x(c_q)
             if live(c_o):
                 quantize_y(c_o)
-            if i == 1:
+            if i == 3:
                 interleave_w_on_gpsimd(0, 0)
                 interleave_w_on_gpsimd(0, 1)
-                interleave_w_on_gpsimd(0, 2)
-                interleave_w_on_gpsimd(0, 3)
-            if i == 3:
+            if i == 4:
+                interleave_w(0, 2, nc.vector.tensor_copy)
+            if i == 5:
+                interleave_w(0, 3, nc.vector.tensor_copy)
                 quantize_w(0, 0)
                 interleave_w_on_gpsimd(1, 0)
                 interleave_w_on_gpsimd(1, 1)
-                interleave_w(1, 2, nc.vector.tensor_copy)
-            if i == 4:
+            if i == 6:
                 quantize_w(0, 1)
+                interleave_w(1, 2, nc.vector.tensor_copy)
+            if i == 7:
                 interleave_w(1, 3, nc.vector.tensor_copy)
-            if i == 5:
                 quantize_w(1, 0)
+            if i == 8:
                 quantize_w(1, 1)
 
             if live(c_z - 1):
@@ -365,8 +365,8 @@ def tile_coil_compress_grappa_planes_k5_kernel(
                 turn_v(i - 1)
             if i == 1:
                 turn_filters()
-            if live(c_x):
-                turn_words(bank_xt, [xb[(2 * c_x + g) % 6] for g in range(2)])
+            if live(c_w):
+                turn_words(bank_xt, [xb[(2 * c_w + g) % 6] for g in range(2)])
             if live(c_t):
                 turn_words(yt_bank(c_t), [yb[(2 * c_t + g) % 8] for g in range(2)])
             if live(c_o):

@@ -12,24 +12,24 @@ FP8X4 = mybir.dt.float8_e4m3fn_x4
 FP4X4 = mybir.dt.float4_e2m1fn_x4
 COPY = mybir.ActivationFunctionType.Copy
 MULT = mybir.AluOpType.mult
-ADD = mybir.AluOpType.add
 
 P = 128
-A_ALL, TAPS, CH, POS, K1 = 2048, 8, 128, 8, 1024
-S_LEN, N_OUT = TAPS * CH, POS * CH
-FLOPS = 2 * K1 * A_ALL * TAPS * CH + 2 * A_ALL * S_LEN * N_OUT
-CHUNKS = A_ALL // P
+HOODS, TAPS, CH, POS, COILS = 2048, 8, 128, 8, 1024
+N_OUT = POS * CH
+FLOPS = 2 * COILS * HOODS * TAPS * CH + 2 * HOODS * TAPS * CH * N_OUT
+CHUNKS = HOODS // P
 ROWS = P * TAPS
 BANK = 512
+QUARTER = N_OUT // 4
 
-LAG = 9
-XQ_RING = LAG - 1
-D_RING, D_AHEAD = 8, 4
-SC_RING = 3
-W_AFTER = [2, 4, 5, 7]
-Y_RING = 5
+LAG = 6
+D_AHEAD = 4
+
+D_RING, SCALE_RING, VT_RING, XB_RING, XG_RING, XQ_RING = 8, 3, 3, 3, 2, LAG - 1
+Y_RING, YB_RING, YG_RING = 5, 4, 3
+
 WORD_GROUPS = [(0, 4), (4, 8), (8, 11), (11, 13), (13, 15), (15, 16)]
-SCALE_GROUPS = [(0, 9), (9, 16)]
+SCALE_GROUPS = [(0, 8), (8, 14), (14, 16)]
 
 
 def tile_coil_compress_grappa_planes_k5_kernel(
@@ -50,7 +50,7 @@ def tile_coil_compress_grappa_planes_k5_kernel(
         bank_xt, bank_yt = banks("bank_xt", 1)[0], banks("bank_yt", 1)[0]
 
         dw = ring("dw", D_RING, [P, 2, 2 * ROWS], U8)
-        dsc = ring("dsc", SC_RING, [P, 2, 2 * ROWS], U8)
+        dsc = ring("dsc", SCALE_RING, [P, 2, 2 * ROWS], U8)
         cw = sb.tile([P, 2, 2 * CH], U8, align_bytes=64)
         csc = sb.tile([P, 2, CH], U8, align_bytes=64)
         ident = sb.tile([P, P], F32, align_bytes=64)
@@ -58,20 +58,20 @@ def tile_coil_compress_grappa_planes_k5_kernel(
         gain_pad = sb.tile([P, CH], F32, align_bytes=64)
         gain_t = sb.tile([P, TAPS, 1], F32, align_bytes=64)
         filt_rows = sb.tile([2 * CHUNKS, ROWS], BF16, align_bytes=64)
-        filt_words = sb.tile([P, 4, P], F32, align_bytes=64)
+        filt_pairs = sb.tile([P, 4, P], F32, align_bytes=64)
         filt = sb.tile([P, 2 * CHUNKS, TAPS], F32, align_bytes=64)
-        w_raw = ring("w_raw", 4, [P, 4, BANK], BF16)
+        w_raw = ring("w_raw", 2, [P, 4, N_OUT], BF16)
         w_grp = ring("w_grp", 4, [P, BANK, 4], BF16)
         wq = ring("wq", 4, [P, BANK], U32)
         ws = ring("ws", 4, [P, BANK], U8)
-        vt = ring("vt", 3, [P, TAPS, P], F32)
-        xb = ring("xb", 6, [P, BANK], BF16)
-        xg = ring("xg", 2, [P, 2 * BANK], BF16)
+        vt = ring("vt", VT_RING, [P, TAPS, P], F32)
+        xb = ring("xb", 2 * XB_RING, [P, BANK], BF16)
+        xg = ring("xg", XG_RING, [P, 2 * BANK], BF16)
         xq = ring("xq", XQ_RING, [P, 2 * P], U32)
         xs = ring("xs", XQ_RING, [P, 2 * P], U8)
         y = ring("y", Y_RING, [P, N_OUT], F32)
-        yb = ring("yb", 8, [P, BANK], BF16)
-        yg = ring("yg", 3, [P, 2 * BANK], BF16)
+        yb = ring("yb", 2 * YB_RING, [P, BANK], BF16)
+        yg = ring("yg", YG_RING, [P, 2 * BANK], BF16)
         yq = [
             sb.tile([P, 2, (hi - lo) * P], U32, name="yq%d" % lo, align_bytes=64) for lo, hi in WORD_GROUPS
         ]
@@ -79,190 +79,48 @@ def tile_coil_compress_grappa_planes_k5_kernel(
             sb.tile([P, 2, (hi - lo) * P], U8, name="ys%d" % lo, align_bytes=64) for lo, hi in SCALE_GROUPS
         ]
 
+        def live(c):
+            return 0 <= c < CHUNKS
+
         def group_of(groups, c):
             return [n for n, grp in enumerate(groups) if grp[0] <= c < grp[1]][0]
 
-        def load_d(c):
-            if c % 2 == 0 and c > 0:
-                load_d_scales(c // 2, [nc.sync] * 4)
-            nc.sync.dma_start(
-                out=dw[c % D_RING][:].bitcast(I32),
-                in_=d_words[:, :, 2 * ROWS * c : 2 * ROWS * (c + 1)].rearrange("g p n -> p g n").bitcast(I32),
-            )
-            if c in W_AFTER:
-                load_w(W_AFTER.index(c))
+        def x_halves(c):
+            return [xb[2 * (c % XB_RING) + g] for g in range(2)]
+
+        def y_halves(c):
+            return [yb[2 * (c % YB_RING) + g] for g in range(2)]
 
         def scale_rows(dram, r):
             return dram.rearrange("g (q r) n -> r q g n", r=4)[r].bitcast(I32)
 
-        def load_d_scales(n, queues):
-            for r, queue in enumerate(queues):
-                queue.dma_start(
-                    out=dsc[n % SC_RING][r:P:32, :, :].bitcast(I32),
-                    in_=scale_rows(d_scales[:, :, 2 * ROWS * n : 2 * ROWS * (n + 1)], r),
-                )
+        def load_plane(plane, dram):
+            for r in range(4):
+                nc.sync.dma_start(out=plane[r:P:32, :, :].bitcast(I32), in_=scale_rows(dram, r))
 
-        def load_filters(queue):
-            queue.dma_start(out=filt_rows[0:CHUNKS, :], in_=source_filter.rearrange("(c a) b -> c (a b)", a=P))
-            queue.dma_start(
+        def load_d_scales(pair):
+            load_plane(dsc[pair % SCALE_RING], d_scales[:, :, 2 * ROWS * pair : 2 * ROWS * (pair + 1)])
+
+        def load_d_words(c):
+            nc.sync.dma_start(
+                out=dw[c % D_RING][:].bitcast(I32),
+                in_=d_words[:, :, 2 * ROWS * c : 2 * ROWS * (c + 1)].rearrange("g p n -> p g n").bitcast(I32),
+            )
+
+        def load_d(c):
+            if c % 2 == 0:
+                load_d_scales(c // 2)
+            load_d_words(c)
+
+        def load_w(g):
+            rows = kernel[BANK * g : BANK * (g + 1), :]
+            nc.sync.dma_start(out=w_raw[g][:], in_=rows.rearrange("(p t) n -> p t n", t=4))
+
+        def load_filters():
+            nc.sync.dma_start(out=filt_rows[0:CHUNKS, :], in_=source_filter.rearrange("(c a) b -> c (a b)", a=P))
+            nc.sync.dma_start(
                 out=filt_rows[CHUNKS : 2 * CHUNKS, :], in_=unfilter.rearrange("(c a) j -> c (a j)", a=P)
             )
-
-        def load_w(n):
-            g, h = divmod(n, 2)
-            rows = kernel[BANK * g : BANK * (g + 1), BANK * h : BANK * (h + 1)]
-            nc.sync.dma_start(out=w_raw[n][:], in_=rows.rearrange("(p t) n -> p t n", t=4))
-
-        def gpsimd_copy(out, in_):
-            nc.gpsimd.tensor_scalar(out=out, in0=in_, scalar1=1.0, scalar2=0.0, op0=MULT, op1=ADD)
-
-        def interleave_w(g, q, copy):
-            h, lo = q // 2, 256 * (q % 2)
-            copy(
-                out=w_grp[2 * g + h][:, lo : lo + 256, :].rearrange("p (c i) t -> p c t i", i=4),
-                in_=w_raw[2 * g + h][:, :, lo : lo + 256].rearrange("p t (c i) -> p c t i", i=4),
-            )
-
-        def interleave_w_on_gpsimd(g, q):
-            for s in range(2):
-                n0 = 256 * q + P * s
-                gpsimd_copy(
-                    out=w_grp[2 * g + q // 2][:, n0 % BANK : n0 % BANK + P, :].rearrange("p (c i) t -> p c t i", i=4),
-                    in_=w_raw[2 * g + q // 2][:, :, n0 % BANK : n0 % BANK + P].rearrange("p t (c i) -> p c t i", i=4),
-                )
-
-        def quantize_w(g, h):
-            n = 2 * g + h
-            nc.vector.quantize_mx(
-                out=wq[n][:].bitcast(FP8X4), scales=ws[n][:], in_=w_grp[n][:].rearrange("p n t -> p (n t)")
-            )
-
-        def v_bank(c, h):
-            return bank_z[h] if c < LAG and c % 2 == 1 else bank_v[h]
-
-        def z_bank(c, h):
-            return bank_v[h] if c + LAG > CHUNKS and c % 2 == 1 else bank_z[h]
-
-        def yt_bank(c):
-            return bank_vt[0] if c + LAG > CHUNKS + 1 and c % 2 == 1 else bank_yt
-
-        def compress(c, h):
-            col = ROWS * (c % 2) + BANK * h
-            for g in range(2):
-                nc.tensor.matmul_mx(
-                    out=v_bank(c, h)[:],
-                    lhsT=cw[:, g, :].bitcast(FP4X4),
-                    lhsT_scale=csc[:, g, :],
-                    rhs=dw[c % D_RING][:, g, 2 * BANK * h : 2 * BANK * (h + 1)].bitcast(FP4X4),
-                    rhs_scale=dsc[c // 2 % SC_RING][:, g, col : col + BANK],
-                    start=(g == 0),
-                    stop=(g == 1),
-                )
-
-        def turn_gain():
-            nc.scalar.activation(out=gain_pad[0:TAPS, :], in_=gain_rows[:], func=COPY)
-            nc.tensor.transpose(bank_xt[:, 0:P], gain_pad[:], ident[:])
-            nc.vector.tensor_copy(out=gain_t[:, :, 0], in_=bank_xt[:, 0:TAPS])
-
-        def sort_filters():
-            nc.vector.tensor_copy(
-                out=filt_words[0 : 2 * CHUNKS], in_=filt_rows[:].bitcast(F32).rearrange("c (a n) -> c n a", n=4)
-            )
-
-        def turn_filters():
-            for n in range(4):
-                nc.tensor.transpose(bank_yt[:, P * n : P * (n + 1)], filt_words[:, n, :], ident[:])
-            nc.vector.tensor_copy(
-                out=filt[:].rearrange("p c (n u) -> p c n u", u=2),
-                in_=bank_yt[:].bitcast(BF16).rearrange("p (n c u) -> p c n u", n=4, u=2)[:, 0 : 2 * CHUNKS],
-            )
-
-        def apply_gain(c, h):
-            nc.vector.tensor_tensor(
-                out=vt[c % 3][:, :, 64 * h : 64 * (h + 1)],
-                in0=v_bank(c, h)[:].rearrange("p (a b) -> p b a", b=TAPS),
-                in1=gain_t[:].to_broadcast([P, TAPS, 64]),
-                op=MULT,
-            )
-
-        def turn_v(c):
-            for b in range(TAPS):
-                nc.tensor.transpose(bank_vt[b // 4][:, P * (b % 4) : P * (b % 4 + 1)], vt[c % 3][:, b, :], ident[:])
-
-        def apply_source_filter(c):
-            for b in range(TAPS):
-                g, b4 = divmod(b, 4)
-                nc.scalar.activation(
-                    out=xb[(2 * c + g) % 6][:].rearrange("p (e b m u) -> p b e m u", e=2, b=4, u=2)[:, b4],
-                    in_=bank_vt[g][:, P * b4 : P * (b4 + 1)].rearrange("p (m e u) -> p e m u", e=2, u=2),
-                    func=COPY,
-                    scale=filt[:, c, b : b + 1],
-                )
-
-        def turn_words(bank, halves):
-            for g in range(2):
-                words = halves[g][:].bitcast(F32)
-                for e in range(2):
-                    n = 2 * g + e
-                    nc.tensor.transpose(bank[:, P * n : P * (n + 1)], words[:, P * e : P * (e + 1)], ident[:])
-
-        def gather_words(copy, dst, bank):
-            copy(
-                out=dst[:].bitcast(F32).rearrange("p (g a e) -> p g a e", g=2, e=2),
-                in_=bank[:].rearrange("p (g e a) -> p g a e", g=2, e=2),
-            )
-
-        def quantize_x(c):
-            nc.vector.quantize_mx(
-                out=xq[c % XQ_RING][:].bitcast(FP8X4), scales=xs[c % XQ_RING][:], in_=xg[c % 2][:]
-            )
-
-        def predict(c, h):
-            for g in range(2):
-                nc.tensor.matmul_mx(
-                    out=z_bank(c, h)[:],
-                    lhsT=xq[c % XQ_RING][:, P * g : P * (g + 1)].bitcast(FP8X4),
-                    lhsT_scale=xs[c % XQ_RING][:, P * g : P * (g + 1)],
-                    rhs=wq[2 * g + h][:].bitcast(FP8X4),
-                    rhs_scale=ws[2 * g + h][:],
-                    start=(g == 0),
-                    stop=(g == 1),
-                )
-
-        def unfilter_on_scalar(c, h):
-            for j4 in range(4):
-                j = 4 * h + j4
-                nc.scalar.activation(
-                    out=y[c % Y_RING][:, CH * j : CH * (j + 1)],
-                    in_=z_bank(c, h)[:, CH * j4 : CH * (j4 + 1)],
-                    func=COPY,
-                    scale=filt[:, CHUNKS + c, j : j + 1],
-                )
-
-        def unfilter_on_vector(c, h):
-            factors = filt[:, CHUNKS + c, 4 * h : 4 * h + 4].rearrange("p (j o) -> p j o", o=1)
-            nc.vector.tensor_tensor(
-                out=y[c % Y_RING][:, BANK * h : BANK * (h + 1)].rearrange("p (j f) -> p j f", j=4),
-                in0=z_bank(c, h)[:].rearrange("p (j f) -> p j f", j=4),
-                in1=factors.to_broadcast([P, 4, CH]),
-                op=MULT,
-            )
-
-        def round_y(c, g):
-            nc.vector.tensor_copy(
-                out=yb[(2 * c + g) % 8][:].rearrange("p (e o i u) -> p o e i u", e=2, i=4, u=2),
-                in_=y[c % Y_RING][:, BANK * g : BANK * (g + 1)].rearrange("p (o i e u) -> p o e i u", e=2, i=4, u=2),
-            )
-
-        def quantize_y(c):
-            nw, ns = group_of(WORD_GROUPS, c), group_of(SCALE_GROUPS, c)
-            cw0, cs0 = P * (c - WORD_GROUPS[nw][0]), P * (c - SCALE_GROUPS[ns][0])
-            for g in range(2):
-                nc.vector.quantize_mx(
-                    out=yq[nw][:, g, cw0 : cw0 + P].bitcast(FP8X4),
-                    scales=ys[ns][:, g, cs0 : cs0 + P],
-                    in_=yg[c % 3][:, BANK * g : BANK * (g + 1)],
-                )
 
         def store_y(c):
             nc.sync.dma_start(out=out_0[P * c : P * (c + 1), :], in_=y[c % Y_RING][:])
@@ -282,8 +140,168 @@ def tile_coil_compress_grappa_planes_k5_kernel(
                         out=scale_rows(out_2[:, :, P * lo : P * hi], r), in_=ys[ns][r:P:32, :, :].bitcast(I32)
                     )
 
-        def live(c):
-            return 0 <= c < CHUNKS
+        def turn_gain():
+            nc.scalar.activation(out=gain_pad[0:TAPS, :], in_=gain_rows[:], func=COPY)
+            nc.tensor.transpose(bank_xt[:, 0:P], gain_pad[:], ident[:])
+            nc.vector.tensor_copy(out=gain_t[:, :, 0], in_=bank_xt[:, 0:TAPS])
+
+        def sort_filters():
+            nc.vector.tensor_copy(
+                out=filt_pairs[0 : 2 * CHUNKS], in_=filt_rows[:].bitcast(F32).rearrange("c (a n) -> c n a", n=4)
+            )
+
+        def turn_filters():
+            for n in range(4):
+                nc.tensor.transpose(bank_yt[:, P * n : P * (n + 1)], filt_pairs[:, n, :], ident[:])
+            nc.vector.tensor_copy(
+                out=filt[:].rearrange("p c (n u) -> p c n u", u=2),
+                in_=bank_yt[:].bitcast(BF16).rearrange("p (n c u) -> p c n u", n=4, u=2)[:, 0 : 2 * CHUNKS],
+            )
+
+        def interleave_w(g, quarter, copy):
+            h, lo = quarter // 2, QUARTER * (quarter % 2)
+            copy(
+                out=w_grp[2 * g + h][:, lo : lo + QUARTER, :].rearrange("p (c i) t -> p c t i", i=4),
+                in_=w_raw[g][:, :, QUARTER * quarter : QUARTER * (quarter + 1)].rearrange("p t (c i) -> p c t i", i=4),
+            )
+
+        def quantize_w(g):
+            for n in (2 * g, 2 * g + 1):
+                nc.vector.quantize_mx(
+                    out=wq[n][:].bitcast(FP8X4), scales=ws[n][:], in_=w_grp[n][:].rearrange("p n t -> p (n t)")
+                )
+
+        def prepare_w(i):
+            if i == 1:
+                interleave_w(0, 0, nc.scalar.copy)
+                interleave_w(0, 1, nc.scalar.copy)
+                interleave_w(0, 2, nc.vector.tensor_copy)
+                interleave_w(0, 3, nc.vector.tensor_copy)
+            if i == 2:
+                quantize_w(0)
+                interleave_w(1, 0, nc.scalar.copy)
+            if i == 3:
+                for quarter in (1, 2, 3):
+                    interleave_w(1, quarter, nc.vector.tensor_copy)
+            if i == 4:
+                quantize_w(1)
+
+        def v_bank(c, h):
+            return bank_z[h] if c < LAG and c % 2 == 1 else bank_v[h]
+
+        def z_bank(c, h):
+            return bank_v[h] if c + LAG > CHUNKS and c % 2 == 1 else bank_z[h]
+
+        def yt_bank(c):
+            return bank_vt[0] if c + LAG > CHUNKS + 1 and c % 2 == 1 else bank_yt
+
+        def compress(c, h):
+            col = ROWS * (c % 2) + BANK * h
+            for g in range(2):
+                nc.tensor.matmul_mx(
+                    out=v_bank(c, h)[:],
+                    lhsT=cw[:, g, :].bitcast(FP4X4),
+                    lhsT_scale=csc[:, g, :],
+                    rhs=dw[c % D_RING][:, g, 2 * BANK * h : 2 * BANK * (h + 1)].bitcast(FP4X4),
+                    rhs_scale=dsc[c // 2 % SCALE_RING][:, g, col : col + BANK],
+                    start=(g == 0),
+                    stop=(g == 1),
+                )
+
+        def apply_gain(c, h):
+            half = P // 2
+            nc.vector.tensor_tensor(
+                out=vt[c % VT_RING][:, :, half * h : half * (h + 1)],
+                in0=v_bank(c, h)[:].rearrange("p (a b) -> p b a", b=TAPS),
+                in1=gain_t[:].to_broadcast([P, TAPS, half]),
+                op=MULT,
+            )
+
+        def turn_v(c):
+            for b in range(TAPS):
+                g, b4 = divmod(b, 4)
+                nc.tensor.transpose(bank_vt[g][:, P * b4 : P * (b4 + 1)], vt[c % VT_RING][:, b, :], ident[:])
+
+        def filter_source(c):
+            for b in range(TAPS):
+                g, b4 = divmod(b, 4)
+                nc.scalar.activation(
+                    out=x_halves(c)[g][:].rearrange("p (e b m u) -> p b e m u", e=2, b=4, u=2)[:, b4],
+                    in_=bank_vt[g][:, P * b4 : P * (b4 + 1)].rearrange("p (m e u) -> p e m u", e=2, u=2),
+                    func=COPY,
+                    scale=filt[:, c, b : b + 1],
+                )
+
+        def turn_pairs(bank, halves):
+            for g in range(2):
+                pairs = halves[g][:].bitcast(F32)
+                for e in range(2):
+                    n = 2 * g + e
+                    nc.tensor.transpose(bank[:, P * n : P * (n + 1)], pairs[:, P * e : P * (e + 1)], ident[:])
+
+        def join_pairs(copy, dst, bank):
+            copy(
+                out=dst[:].bitcast(F32).rearrange("p (g a e) -> p g a e", g=2, e=2),
+                in_=bank[:].rearrange("p (g e a) -> p g a e", g=2, e=2),
+            )
+
+        def join_pairs_by_group(dst, bank):
+            for g in range(2):
+                nc.scalar.copy(
+                    out=dst[:, BANK * g : BANK * (g + 1)].bitcast(F32).rearrange("p (a e) -> p a e", e=2),
+                    in_=bank[:, 2 * P * g : 2 * P * (g + 1)].rearrange("p (e a) -> p a e", e=2),
+                )
+
+        def quantize_x(c):
+            nc.vector.quantize_mx(
+                out=xq[c % XQ_RING][:].bitcast(FP8X4), scales=xs[c % XQ_RING][:], in_=xg[c % XG_RING][:]
+            )
+
+        def predict(c, h):
+            for g in range(2):
+                nc.tensor.matmul_mx(
+                    out=z_bank(c, h)[:],
+                    lhsT=xq[c % XQ_RING][:, P * g : P * (g + 1)].bitcast(FP8X4),
+                    lhsT_scale=xs[c % XQ_RING][:, P * g : P * (g + 1)],
+                    rhs=wq[2 * g + h][:].bitcast(FP8X4),
+                    rhs_scale=ws[2 * g + h][:],
+                    start=(g == 0),
+                    stop=(g == 1),
+                )
+
+        def undo_filter(c):
+            for j in range(4):
+                nc.scalar.activation(
+                    out=y[c % Y_RING][:, CH * j : CH * (j + 1)],
+                    in_=z_bank(c, 0)[:, CH * j : CH * (j + 1)],
+                    func=COPY,
+                    scale=filt[:, CHUNKS + c, j : j + 1],
+                )
+            factors = filt[:, CHUNKS + c, 4:POS].rearrange("p (j o) -> p j o", o=1)
+            nc.vector.tensor_tensor(
+                out=y[c % Y_RING][:, BANK:N_OUT].rearrange("p (j f) -> p j f", j=4),
+                in0=z_bank(c, 1)[:].rearrange("p (j f) -> p j f", j=4),
+                in1=factors.to_broadcast([P, 4, CH]),
+                op=MULT,
+            )
+
+        def round_y(c):
+            for g in range(2):
+                cols = y[c % Y_RING][:, BANK * g : BANK * (g + 1)]
+                nc.vector.tensor_copy(
+                    out=y_halves(c)[g][:].rearrange("p (e o i u) -> p o e i u", e=2, i=4, u=2),
+                    in_=cols.rearrange("p (o i e u) -> p o e i u", e=2, i=4, u=2),
+                )
+
+        def quantize_y(c):
+            nw, ns = group_of(WORD_GROUPS, c), group_of(SCALE_GROUPS, c)
+            word0, scale0 = P * (c - WORD_GROUPS[nw][0]), P * (c - SCALE_GROUPS[ns][0])
+            for g in range(2):
+                nc.vector.quantize_mx(
+                    out=yq[nw][:, g, word0 : word0 + P].bitcast(FP8X4),
+                    scales=ys[ns][:, g, scale0 : scale0 + P],
+                    in_=yg[c % YG_RING][:, BANK * g : BANK * (g + 1)],
+                )
 
         ctx.enter_context(tc.manual_schedule())
 
@@ -291,39 +309,40 @@ def tile_coil_compress_grappa_planes_k5_kernel(
         nc.vector.memset(dsc[0][:].bitcast(I32), 0)
         nc.vector.memset(gain_pad[:], 0.0)
         nc.vector.memset(dsc[1][:].bitcast(I32), 0)
-        nc.vector.memset(filt_words[32:64], 0.0)
-        nc.vector.memset(filt_words[64:P], 0.0)
+        nc.vector.memset(filt_pairs[32:64], 0.0)
+        nc.vector.memset(filt_pairs[64:P], 0.0)
         nc.vector.memset(dsc[2][:].bitcast(I32), 0)
         make_identity(nc, ident[:])
+
         nc.sync.dma_start(out=cw[:].bitcast(I32), in_=c_words.rearrange("g p n -> p g n").bitcast(I32))
         nc.sync.dma_start(out=gain_rows[:], in_=gain[:, :])
-        for r in range(4):
-            nc.sync.dma_start(out=csc[r:P:32, :, :].bitcast(I32), in_=scale_rows(c_scales, r))
-        load_d(0)
-        load_d_scales(0, [nc.sync] * 4)
+        load_plane(csc, c_scales)
+        load_d_words(0)
+        load_d_scales(0)
         load_d(1)
-
-        load_filters(nc.sync)
-        for c in range(2, D_AHEAD):
+        load_w(0)
+        load_filters()
+        load_d(2)
+        load_w(1)
+        for c in range(3, D_AHEAD):
             load_d(c)
-
         turn_gain()
 
-        for i in range(CHUNKS + LAG + 1 + 1):
-            c_x, c_w, c_q, c_z = i - 2, i - 3, i - 4, i - LAG
-            c_t, c_o = c_z - 1, c_z - 1 - 1
+        for i in range(CHUNKS + LAG + 2):
+            c_v, c_x, c_q = i - 1, i - 2, i - 3
+            c_z, c_y, c_o = i - LAG, i - LAG - 1, i - LAG - 2
             if live(i + D_AHEAD):
                 load_d(i + D_AHEAD)
-
             if live(c_x):
-                apply_source_filter(c_x)
+                filter_source(c_x)
             if live(c_q):
-                gather_words(nc.scalar.copy, xg[c_q % 2], bank_xt)
-            if live(c_o):
-                gather_words(nc.scalar.copy, yg[c_o % 3], yt_bank(c_o))
-            if live(c_z - 1):
-                round_y(c_z - 1, 0)
-                round_y(c_z - 1, 1)
+                join_pairs(nc.scalar.copy if live(i) else nc.vector.tensor_copy, xg[c_q % XG_RING], bank_xt)
+            if c_o == CHUNKS - 1:
+                join_pairs_by_group(yg[c_o % YG_RING], yt_bank(c_o))
+            elif live(c_o):
+                join_pairs(nc.scalar.copy, yg[c_o % YG_RING], yt_bank(c_o))
+            if live(c_y):
+                round_y(c_y)
             if live(i):
                 compress(i, 0)
                 compress(i, 1)
@@ -335,39 +354,20 @@ def tile_coil_compress_grappa_planes_k5_kernel(
                 quantize_x(c_q)
             if live(c_o):
                 quantize_y(c_o)
-            if i == 3:
-                interleave_w_on_gpsimd(0, 0)
-                interleave_w_on_gpsimd(0, 1)
-            if i == 4:
-                interleave_w(0, 2, nc.vector.tensor_copy)
-            if i == 5:
-                interleave_w(0, 3, nc.vector.tensor_copy)
-                quantize_w(0, 0)
-                interleave_w_on_gpsimd(1, 0)
-                interleave_w_on_gpsimd(1, 1)
-            if i == 6:
-                quantize_w(0, 1)
-                interleave_w(1, 2, nc.vector.tensor_copy)
-            if i == 7:
-                interleave_w(1, 3, nc.vector.tensor_copy)
-                quantize_w(1, 0)
-            if i == 8:
-                quantize_w(1, 1)
-
-            if live(c_z - 1):
-                store_y(c_z - 1)
+            prepare_w(i)
+            if live(c_y):
+                store_y(c_y)
             if live(c_z):
                 predict(c_z, 0)
                 predict(c_z, 1)
-                unfilter_on_scalar(c_z, 0)
-                unfilter_on_vector(c_z, 1)
-            if live(i - 1):
-                turn_v(i - 1)
+                undo_filter(c_z)
+            if live(c_v):
+                turn_v(c_v)
             if i == 1:
                 turn_filters()
-            if live(c_w):
-                turn_words(bank_xt, [xb[(2 * c_w + g) % 6] for g in range(2)])
-            if live(c_t):
-                turn_words(yt_bank(c_t), [yb[(2 * c_t + g) % 8] for g in range(2)])
+            if live(c_x):
+                turn_pairs(bank_xt, x_halves(c_x))
+            if live(c_y):
+                turn_pairs(yt_bank(c_y), y_halves(c_y))
             if live(c_o):
                 store_planes(c_o)

from contextlib import ExitStack

import concourse.mybir as mybir
from concourse.masks import make_identity

F32 = mybir.dt.float32
BF16 = mybir.dt.bfloat16
U32 = mybir.dt.uint32
I32 = mybir.dt.int32
U8 = mybir.dt.uint8
FP8X4 = mybir.dt.float8_e4m3fn_x4
FP4X4 = mybir.dt.float4_e2m1fn_x4
COPY = mybir.ActivationFunctionType.Copy
MULT = mybir.AluOpType.mult

P = 128
HOODS, TAPS, CH, POS, COILS = 2048, 8, 128, 8, 1024
N_OUT = POS * CH
FLOPS = 2 * COILS * HOODS * TAPS * CH + 2 * HOODS * TAPS * CH * N_OUT
CHUNKS = HOODS // P
ROWS = P * TAPS
BANK = 512
QUARTER = N_OUT // 4

LAG = 6
D_AHEAD = 4

D_RING, SCALE_RING, VT_RING, XB_RING, XG_RING, XQ_RING = 8, 3, 3, 3, 2, LAG - 1
Y_RING, YB_RING, YG_RING = 5, 4, 3

WORD_GROUPS = [(0, 4), (4, 8), (8, 11), (11, 13), (13, 15), (15, 16)]
SCALE_GROUPS = [(0, 8), (8, 14), (14, 16)]


def tile_coil_compress_grappa_planes_k5_kernel(
    tc, d_words, d_scales, c_words, c_scales, source_filter, gain, kernel, unfilter, out_0, out_1, out_2
):
    nc = tc.nc
    with ExitStack() as ctx:
        sb = ctx.enter_context(tc.tile_pool(name="sb", bufs=1))
        ps = ctx.enter_context(tc.psum_pool(name="ps", bufs=1))

        def ring(name, count, shape, dtype):
            return [sb.tile(shape, dtype, name="%s%d" % (name, n), align_bytes=64) for n in range(count)]

        def banks(name, count):
            return [ps.tile([P, BANK], F32, name="%s%d" % (name, n)) for n in range(count)]

        bank_v, bank_vt, bank_z = banks("bank_v", 2), banks("bank_vt", 2), banks("bank_z", 2)
        bank_xt, bank_yt = banks("bank_xt", 1)[0], banks("bank_yt", 1)[0]

        dw = ring("dw", D_RING, [P, 2, 2 * ROWS], U8)
        dsc = ring("dsc", SCALE_RING, [P, 2, 2 * ROWS], U8)
        cw = sb.tile([P, 2, 2 * CH], U8, align_bytes=64)
        csc = sb.tile([P, 2, CH], U8, align_bytes=64)
        ident = sb.tile([P, P], F32, align_bytes=64)
        gain_rows = sb.tile([TAPS, CH], BF16, align_bytes=64)
        gain_pad = sb.tile([P, CH], F32, align_bytes=64)
        gain_t = sb.tile([P, TAPS, 1], F32, align_bytes=64)
        filt_rows = sb.tile([2 * CHUNKS, ROWS], BF16, align_bytes=64)
        filt_pairs = sb.tile([P, 4, P], F32, align_bytes=64)
        filt = sb.tile([P, 2 * CHUNKS, TAPS], F32, align_bytes=64)
        w_raw = ring("w_raw", 2, [P, 4, N_OUT], BF16)
        w_grp = ring("w_grp", 4, [P, BANK, 4], BF16)
        wq = ring("wq", 4, [P, BANK], U32)
        ws = ring("ws", 4, [P, BANK], U8)
        vt = ring("vt", VT_RING, [P, TAPS, P], F32)
        xb = ring("xb", 2 * XB_RING, [P, BANK], BF16)
        xg = ring("xg", XG_RING, [P, 2 * BANK], BF16)
        xq = ring("xq", XQ_RING, [P, 2 * P], U32)
        xs = ring("xs", XQ_RING, [P, 2 * P], U8)
        y = ring("y", Y_RING, [P, N_OUT], F32)
        yb = ring("yb", 2 * YB_RING, [P, BANK], BF16)
        yg = ring("yg", YG_RING, [P, 2 * BANK], BF16)
        yq = [
            sb.tile([P, 2, (hi - lo) * P], U32, name="yq%d" % lo, align_bytes=64) for lo, hi in WORD_GROUPS
        ]
        ys = [
            sb.tile([P, 2, (hi - lo) * P], U8, name="ys%d" % lo, align_bytes=64) for lo, hi in SCALE_GROUPS
        ]

        def live(c):
            return 0 <= c < CHUNKS

        def group_of(groups, c):
            return [n for n, grp in enumerate(groups) if grp[0] <= c < grp[1]][0]

        def x_halves(c):
            return [xb[2 * (c % XB_RING) + g] for g in range(2)]

        def y_halves(c):
            return [yb[2 * (c % YB_RING) + g] for g in range(2)]

        def scale_rows(dram, r):
            return dram.rearrange("g (q r) n -> r q g n", r=4)[r].bitcast(I32)

        def load_plane(plane, dram):
            for r in range(4):
                nc.sync.dma_start(out=plane[r:P:32, :, :].bitcast(I32), in_=scale_rows(dram, r))

        def load_d_scales(pair):
            load_plane(dsc[pair % SCALE_RING], d_scales[:, :, 2 * ROWS * pair : 2 * ROWS * (pair + 1)])

        def load_d_words(c):
            nc.sync.dma_start(
                out=dw[c % D_RING][:].bitcast(I32),
                in_=d_words[:, :, 2 * ROWS * c : 2 * ROWS * (c + 1)].rearrange("g p n -> p g n").bitcast(I32),
            )

        def load_d(c):
            if c % 2 == 0:
                load_d_scales(c // 2)
            load_d_words(c)

        def load_w(g):
            rows = kernel[BANK * g : BANK * (g + 1), :]
            nc.sync.dma_start(out=w_raw[g][:], in_=rows.rearrange("(p t) n -> p t n", t=4))

        def load_filters():
            nc.sync.dma_start(out=filt_rows[0:CHUNKS, :], in_=source_filter.rearrange("(c a) b -> c (a b)", a=P))
            nc.sync.dma_start(
                out=filt_rows[CHUNKS : 2 * CHUNKS, :], in_=unfilter.rearrange("(c a) j -> c (a j)", a=P)
            )

        def store_y(c):
            nc.sync.dma_start(out=out_0[P * c : P * (c + 1), :], in_=y[c % Y_RING][:])

        def store_planes(c):
            nw, ns = group_of(WORD_GROUPS, c), group_of(SCALE_GROUPS, c)
            lo, hi = WORD_GROUPS[nw]
            if c == hi - 1:
                nc.sync.dma_start(
                    out=out_1[:, :, P * lo : P * hi, :].rearrange("g p m t -> p g (m t)").bitcast(I32),
                    in_=yq[nw][:].bitcast(I32),
                )
            lo, hi = SCALE_GROUPS[ns]
            if c == hi - 1:
                for r in range(4):
                    nc.sync.dma_start(
                        out=scale_rows(out_2[:, :, P * lo : P * hi], r), in_=ys[ns][r:P:32, :, :].bitcast(I32)
                    )

        def turn_gain():
            nc.scalar.activation(out=gain_pad[0:TAPS, :], in_=gain_rows[:], func=COPY)
            nc.tensor.transpose(bank_xt[:, 0:P], gain_pad[:], ident[:])
            nc.vector.tensor_copy(out=gain_t[:, :, 0], in_=bank_xt[:, 0:TAPS])

        def sort_filters():
            nc.vector.tensor_copy(
                out=filt_pairs[0 : 2 * CHUNKS], in_=filt_rows[:].bitcast(F32).rearrange("c (a n) -> c n a", n=4)
            )

        def turn_filters():
            for n in range(4):
                nc.tensor.transpose(bank_yt[:, P * n : P * (n + 1)], filt_pairs[:, n, :], ident[:])
            nc.vector.tensor_copy(
                out=filt[:].rearrange("p c (n u) -> p c n u", u=2),
                in_=bank_yt[:].bitcast(BF16).rearrange("p (n c u) -> p c n u", n=4, u=2)[:, 0 : 2 * CHUNKS],
            )

        def interleave_w(g, quarter, copy):
            h, lo = quarter // 2, QUARTER * (quarter % 2)
            copy(
                out=w_grp[2 * g + h][:, lo : lo + QUARTER, :].rearrange("p (c i) t -> p c t i", i=4),
                in_=w_raw[g][:, :, QUARTER * quarter : QUARTER * (quarter + 1)].rearrange("p t (c i) -> p c t i", i=4),
            )

        def quantize_w(g):
            for n in (2 * g, 2 * g + 1):
                nc.vector.quantize_mx(
                    out=wq[n][:].bitcast(FP8X4), scales=ws[n][:], in_=w_grp[n][:].rearrange("p n t -> p (n t)")
                )

        def prepare_w(i):
            if i == 1:
                interleave_w(0, 0, nc.scalar.copy)
                interleave_w(0, 1, nc.scalar.copy)
                interleave_w(0, 2, nc.vector.tensor_copy)
                interleave_w(0, 3, nc.vector.tensor_copy)
            if i == 2:
                quantize_w(0)
                interleave_w(1, 0, nc.scalar.copy)
            if i == 3:
                for quarter in (1, 2, 3):
                    interleave_w(1, quarter, nc.vector.tensor_copy)
            if i == 4:
                quantize_w(1)

        def v_bank(c, h):
            return bank_z[h] if c < LAG and c % 2 == 1 else bank_v[h]

        def z_bank(c, h):
            return bank_v[h] if c + LAG > CHUNKS and c % 2 == 1 else bank_z[h]

        def yt_bank(c):
            return bank_vt[0] if c + LAG > CHUNKS + 1 and c % 2 == 1 else bank_yt

        def compress(c, h):
            col = ROWS * (c % 2) + BANK * h
            for g in range(2):
                nc.tensor.matmul_mx(
                    out=v_bank(c, h)[:],
                    lhsT=cw[:, g, :].bitcast(FP4X4),
                    lhsT_scale=csc[:, g, :],
                    rhs=dw[c % D_RING][:, g, 2 * BANK * h : 2 * BANK * (h + 1)].bitcast(FP4X4),
                    rhs_scale=dsc[c // 2 % SCALE_RING][:, g, col : col + BANK],
                    start=(g == 0),
                    stop=(g == 1),
                )

        def apply_gain(c, h):
            half = P // 2
            nc.vector.tensor_tensor(
                out=vt[c % VT_RING][:, :, half * h : half * (h + 1)],
                in0=v_bank(c, h)[:].rearrange("p (a b) -> p b a", b=TAPS),
                in1=gain_t[:].to_broadcast([P, TAPS, half]),
                op=MULT,
            )

        def turn_v(c):
            for b in range(TAPS):
                g, b4 = divmod(b, 4)
                nc.tensor.transpose(bank_vt[g][:, P * b4 : P * (b4 + 1)], vt[c % VT_RING][:, b, :], ident[:])

        def filter_source(c):
            for b in range(TAPS):
                g, b4 = divmod(b, 4)
                nc.scalar.activation(
                    out=x_halves(c)[g][:].rearrange("p (e b m u) -> p b e m u", e=2, b=4, u=2)[:, b4],
                    in_=bank_vt[g][:, P * b4 : P * (b4 + 1)].rearrange("p (m e u) -> p e m u", e=2, u=2),
                    func=COPY,
                    scale=filt[:, c, b : b + 1],
                )

        def turn_pairs(bank, halves):
            for g in range(2):
                pairs = halves[g][:].bitcast(F32)
                for e in range(2):
                    n = 2 * g + e
                    nc.tensor.transpose(bank[:, P * n : P * (n + 1)], pairs[:, P * e : P * (e + 1)], ident[:])

        def join_pairs(copy, dst, bank):
            copy(
                out=dst[:].bitcast(F32).rearrange("p (g a e) -> p g a e", g=2, e=2),
                in_=bank[:].rearrange("p (g e a) -> p g a e", g=2, e=2),
            )

        def join_pairs_by_group(dst, bank):
            for g in range(2):
                nc.scalar.copy(
                    out=dst[:, BANK * g : BANK * (g + 1)].bitcast(F32).rearrange("p (a e) -> p a e", e=2),
                    in_=bank[:, 2 * P * g : 2 * P * (g + 1)].rearrange("p (e a) -> p a e", e=2),
                )

        def quantize_x(c):
            nc.vector.quantize_mx(
                out=xq[c % XQ_RING][:].bitcast(FP8X4), scales=xs[c % XQ_RING][:], in_=xg[c % XG_RING][:]
            )

        def predict(c, h):
            for g in range(2):
                nc.tensor.matmul_mx(
                    out=z_bank(c, h)[:],
                    lhsT=xq[c % XQ_RING][:, P * g : P * (g + 1)].bitcast(FP8X4),
                    lhsT_scale=xs[c % XQ_RING][:, P * g : P * (g + 1)],
                    rhs=wq[2 * g + h][:].bitcast(FP8X4),
                    rhs_scale=ws[2 * g + h][:],
                    start=(g == 0),
                    stop=(g == 1),
                )

        def undo_filter(c):
            for j in range(4):
                nc.scalar.activation(
                    out=y[c % Y_RING][:, CH * j : CH * (j + 1)],
                    in_=z_bank(c, 0)[:, CH * j : CH * (j + 1)],
                    func=COPY,
                    scale=filt[:, CHUNKS + c, j : j + 1],
                )
            factors = filt[:, CHUNKS + c, 4:POS].rearrange("p (j o) -> p j o", o=1)
            nc.vector.tensor_tensor(
                out=y[c % Y_RING][:, BANK:N_OUT].rearrange("p (j f) -> p j f", j=4),
                in0=z_bank(c, 1)[:].rearrange("p (j f) -> p j f", j=4),
                in1=factors.to_broadcast([P, 4, CH]),
                op=MULT,
            )

        def round_y(c):
            for g in range(2):
                cols = y[c % Y_RING][:, BANK * g : BANK * (g + 1)]
                nc.vector.tensor_copy(
                    out=y_halves(c)[g][:].rearrange("p (e o i u) -> p o e i u", e=2, i=4, u=2),
                    in_=cols.rearrange("p (o i e u) -> p o e i u", e=2, i=4, u=2),
                )

        def quantize_y(c):
            nw, ns = group_of(WORD_GROUPS, c), group_of(SCALE_GROUPS, c)
            word0, scale0 = P * (c - WORD_GROUPS[nw][0]), P * (c - SCALE_GROUPS[ns][0])
            for g in range(2):
                nc.vector.quantize_mx(
                    out=yq[nw][:, g, word0 : word0 + P].bitcast(FP8X4),
                    scales=ys[ns][:, g, scale0 : scale0 + P],
                    in_=yg[c % YG_RING][:, BANK * g : BANK * (g + 1)],
                )

        ctx.enter_context(tc.manual_schedule())

        nc.vector.memset(csc[:].bitcast(I32), 0)
        nc.vector.memset(dsc[0][:].bitcast(I32), 0)
        nc.vector.memset(gain_pad[:], 0.0)
        nc.vector.memset(dsc[1][:].bitcast(I32), 0)
        nc.vector.memset(filt_pairs[32:64], 0.0)
        nc.vector.memset(filt_pairs[64:P], 0.0)
        nc.vector.memset(dsc[2][:].bitcast(I32), 0)
        make_identity(nc, ident[:])

        nc.sync.dma_start(out=cw[:].bitcast(I32), in_=c_words.rearrange("g p n -> p g n").bitcast(I32))
        nc.sync.dma_start(out=gain_rows[:], in_=gain[:, :])
        load_plane(csc, c_scales)
        load_d_words(0)
        load_d_scales(0)
        load_d(1)
        load_w(0)
        load_filters()
        load_d(2)
        load_w(1)
        for c in range(3, D_AHEAD):
            load_d(c)
        turn_gain()

        for i in range(CHUNKS + LAG + 2):
            c_v, c_x, c_q = i - 1, i - 2, i - 3
            c_z, c_y, c_o = i - LAG, i - LAG - 1, i - LAG - 2
            if live(i + D_AHEAD):
                load_d(i + D_AHEAD)
            if live(c_x):
                filter_source(c_x)
            if live(c_q):
                join_pairs(nc.scalar.copy if live(i) else nc.vector.tensor_copy, xg[c_q % XG_RING], bank_xt)
            if c_o == CHUNKS - 1:
                join_pairs_by_group(yg[c_o % YG_RING], yt_bank(c_o))
            elif live(c_o):
                join_pairs(nc.scalar.copy, yg[c_o % YG_RING], yt_bank(c_o))
            if live(c_y):
                round_y(c_y)
            if live(i):
                compress(i, 0)
                compress(i, 1)
                apply_gain(i, 0)
                apply_gain(i, 1)
            if i == 0:
                sort_filters()
            if live(c_q):
                quantize_x(c_q)
            if live(c_o):
                quantize_y(c_o)
            prepare_w(i)
            if live(c_y):
                store_y(c_y)
            if live(c_z):
                predict(c_z, 0)
                predict(c_z, 1)
                undo_filter(c_z)
            if live(c_v):
                turn_v(c_v)
            if i == 1:
                turn_filters()
            if live(c_x):
                turn_pairs(bank_xt, x_halves(c_x))
            if live(c_y):
                turn_pairs(yt_bank(c_y), y_halves(c_y))
            if live(c_o):
                store_planes(c_o)
